import numpy as np
import ml_dtypes


def mxq(x, axis, fmt="e4m3"):
    dtype, down = {"e4m3": (ml_dtypes.float8_e4m3fn, 7), "e5m2": (ml_dtypes.float8_e5m2, 14)}[fmt]
    v = np.moveaxis(np.asarray(x, np.float32).astype(ml_dtypes.bfloat16).astype(np.float64), axis, -1)
    blocks = v.reshape(v.shape[:-1] + (-1, 32))
    amax = np.abs(blocks).max(-1, keepdims=True)
    byte = np.maximum(np.where(amax > 0, np.frexp(amax)[1] - 1 + 127, 0) - down, 1)
    scale = np.exp2(byte - 127.0)
    codes = (blocks / scale).astype(np.float32).astype(dtype).astype(np.float64)
    return np.moveaxis((codes * scale).reshape(v.shape), -1, axis)


WIDE = False


def mx_kscale(k):
    if not WIDE:
        return np.ones(k)
    levels = np.array([10, -10, 5, -5, 0])
    if k % 512:
        return np.exp2(np.random.permutation(np.resize(levels, k // 32))).repeat(32)
    a = np.empty((k // 512, 16))
    for p in range(k // 512):
        a[p, :8] = np.random.permutation(np.resize(levels, 8))
        for g in range(8):
            far = levels[np.abs(levels - a[p, g]) >= 10]
            a[p, g + 8] = far[np.random.randint(len(far))]
    return np.exp2(a.ravel()).repeat(32)


def f64(x):
    return np.asarray(x).astype(np.float64)


def striped8(idx):
    return np.concatenate([v.reshape(-1, 16).T for v in idx]).astype(np.uint16)


def unstriped8(offs):
    return np.stack([offs[16 * g:16 * g + 16].T.reshape(-1) for g in range(8)]).astype(np.int64)


E2M1 = np.array([0.0, 0.5, 1.0, 1.5, 2.0, 3.0, 4.0, 6.0, -0.0, -0.5, -1.0, -1.5, -2.0, -3.0, -4.0, -6.0])


def pack_weight(w, fmt):
    k, n = w.shape
    w = f64(np.asarray(w, np.float32).astype(ml_dtypes.bfloat16)).reshape(k // 32, 32, n)
    amax = np.abs(w).max(1)
    if fmt == "e4m3":
        byte = np.frexp(amax)[1] - 1 + 127 - 7
    else:
        mant, ex = np.frexp(amax / 6.0)
        byte = np.where(mant > 0.5, ex, ex - 1) + 127
    byte = np.clip(np.where(amax > 0, byte, 1), 1, 254)
    scaled = (w * np.exp2(127.0 - byte)[:, None, :]).reshape(k, n).astype(np.float32)
    by_word = np.ascontiguousarray(scaled.reshape(k // 512, 128, 4, n).transpose(0, 1, 3, 2))
    if fmt == "e4m3":
        words = by_word.astype(ml_dtypes.float8_e4m3fn).view(np.uint8)
    else:
        c = by_word.astype(ml_dtypes.float4_e2m1fn).view(np.uint8) & 0xF
        words = (c[..., 0::2] | (c[..., 1::2] << 4)).reshape(k // 512, 128, 2 * n)
    return np.ascontiguousarray(words), np.ascontiguousarray(byte.astype(np.uint8).reshape(k // 512, 16, n))


def unpack_weight(words, scales, fmt):
    g, _, n = scales.shape
    words = np.ascontiguousarray(words).reshape(g, 128, n, -1)
    if fmt == "e4m3":
        vals = words.view(ml_dtypes.float8_e4m3fn).astype(np.float64)
    else:
        nib = np.empty((g, 128, n, 4), np.uint8)
        nib[..., 0::2] = words & 0xF
        nib[..., 1::2] = words >> 4
        vals = E2M1[nib]
    vals = vals * np.repeat(np.exp2(scales.astype(np.float64) - 127.0), 8, axis=1)[..., None]
    return vals.transpose(0, 1, 3, 2).reshape(g * 512, n)


def silu(v):
    return v / (1.0 + np.exp(-np.maximum(v, -700.0)))


K, M, T, S = 1536, 128, 1024, 512


def setup_inputs():
    n = np.random.standard_normal
    s = mx_kscale(K)[:, None]
    s2 = mx_kscale(512)[:, None]
    p_w4 = pack_weight(n((K, M)) / np.sqrt(K) / s, "e2m1")
    return {
        "x": (n((K, S)) * s).astype(np.float32),
        "w4_words": p_w4[0],
        "w4_scales": p_w4[1],
        "c": (n((512, S)) * s2).astype(np.float32),
        "u": (n((512, M)) / np.sqrt(512) / s2).astype(np.float32),
        "b": (0.3 * n(128)).astype(np.float32),
        "wgo": np.repeat(np.random.uniform(0.5, 2.0, (8, S)), 16, axis=0).astype(np.float32),
        "offs": striped8(np.stack([np.random.permutation(T)[:S] for _ in range(8)])),
    }


def reference(x, w4_words, w4_scales, c, u, b, wgo, offs):
    x_ = mxq(f64(x), 0, "e4m3")
    w4_ = unpack_weight(w4_words, w4_scales, "e2m1")
    c_ = mxq(f64(c), 0, "e4m3")
    u_ = mxq(f64(u), 0, "e4m3")
    y = w4_.T @ x_ + u_.T @ c_
    place = unstriped8(offs)[np.arange(M) % 128 // 16]
    out = np.zeros((M, T))
    out[np.arange(M)[:, None], place] = f64(wgo)[np.arange(M) % 128] * (silu(y + f64(b)[:, None]))
    return out

@@ -1,0 +1,133 @@
+from contextlib import ExitStack
+
+import concourse.mybir as mybir
+
+K, L, M, T, S = 1536, 512, 128, 1024, 512
+FLOPS = 2 * (K + L) * M * S
+
+F32 = mybir.dt.float32
+BF16 = mybir.dt.bfloat16
+I32 = mybir.dt.int32
+U32 = mybir.dt.uint32
+U16 = mybir.dt.uint16
+U8 = mybir.dt.uint8
+FP8X4 = mybir.dt.float8_e4m3fn_x4
+FP4X4 = mybir.dt.float4_e2m1fn_x4
+SILU = mybir.ActivationFunctionType.Silu
+
+P = 128
+PACK = 4
+K_PASS = P * PACK
+X_PASSES = K // K_PASS
+N = 128
+RUN = 4
+
+
+def tile_list_hscat_d_silu_kernel(tc, x, w4_words, w4_scales, c, u, b, wgo, offs, out):
+    nc = tc.nc
+    with ExitStack() as ctx:
+        sb = ctx.enter_context(tc.tile_pool(name="sb", bufs=1))
+        ps = ctx.enter_context(tc.psum_pool(name="ps", bufs=1))
+
+        def load_rows(rows, name):
+            raw = sb.tile([P, PACK, rows.shape[1]], F32, name="raw_" + name, align_bytes=64)
+            nc.sync.dma_start(out=raw[:], in_=rows.rearrange("(p t) w -> p t w", t=PACK))
+            return raw
+
+        def quantise(raw, name, on_vector):
+            width = raw.shape[2]
+            woven = sb.tile([P, width * PACK], BF16, name="woven_" + name, align_bytes=64)
+            for copy, c0, c1 in ((nc.vector.tensor_copy, 0, on_vector), (nc.scalar.copy, on_vector, width)):
+                if c1 > c0:
+                    copy(
+                        out=woven[:, c0 * PACK : c1 * PACK].rearrange("p (w i t) -> p w t i", i=RUN, t=PACK),
+                        in_=raw[:, :, c0:c1].rearrange("p t (w i) -> p w t i", i=RUN),
+                    )
+            codes = sb.tile([P, width], U32, name="codes_" + name, align_bytes=64)
+            scales = sb.tile([P, width], U8, name="scales_" + name, align_bytes=64)
+            nc.vector.quantize_mx(out=codes[:].bitcast(FP8X4), scales=scales[:], in_=woven[:])
+            return codes, scales
+
+        w4_plane = sb.tile([P, X_PASSES, M], U8, name="w4_plane", align_bytes=64)
+        nc.vector.memset(w4_plane[:].bitcast(I32), 0)
+        placed = sb.tile([P, T], F32, name="placed")
+        nc.vector.memset(placed[:], 0.0)
+        warm = sb.tile([P, 1], F32, name="warm")
+        nc.scalar.activation(warm[:], placed[:, 0:1], SILU)
+
+        def x_rows(a, c0, c1):
+            return x[a * K_PASS : (a + 1) * K_PASS, c0:c1]
+
+        raws = {}
+        u_raw = load_rows(u, "u")
+        raws[(0, 0)] = load_rows(c[:, 0:256], "0_0")
+        raws[(1, 0)] = load_rows(x_rows(0, 0, 256), "1_0")
+        for q in range(4):
+            nc.sync.dma_start(
+                out=w4_plane[32 * q : 32 * q + 4, :, :].bitcast(I32),
+                in_=w4_scales[:, 4 * q : 4 * q + 4, :].rearrange("a r n -> r a n").bitcast(I32),
+            )
+        raws[(2, 0)] = load_rows(x_rows(1, 0, 256), "2_0")
+        raws[(3, 0)] = load_rows(x_rows(2, 0, 256), "3_0")
+        w4 = sb.tile([P, X_PASSES, 2 * M], U8, name="w4", align_bytes=64)
+        nc.sync.dma_start(out=w4[:].bitcast(I32), in_=w4_words.rearrange("a p n -> p a n").bitcast(I32))
+        bias = sb.tile([P, 1], F32, name="bias")
+        nc.sync.dma_start(out=bias[:], in_=b.rearrange("(p o) -> p o", o=1))
+        offsets = sb.tile([P, S // 16], U16, name="offsets")
+        nc.sync.dma_start(offsets[:], offs)
+        wgo_a = sb.tile([P, 256], F32, name="wgo_a")
+        nc.sync.dma_start(out=wgo_a[:], in_=wgo[:, 0:256])
+        raws[(0, 256)] = load_rows(c[:, 256:512], "0_256")
+        raws[(1, 256)] = load_rows(x_rows(0, 256, 512), "1_256")
+        raws[(2, 256)] = load_rows(x_rows(1, 256, 384), "2_256")
+        raws[(3, 256)] = load_rows(x_rows(2, 256, 384), "3_256")
+        raws[(2, 384)] = load_rows(x_rows(1, 384, 512), "2_384")
+        raws[(3, 384)] = load_rows(x_rows(2, 384, 512), "3_384")
+        wgo_b = sb.tile([P, 256], F32, name="wgo_b")
+        nc.sync.dma_start(out=wgo_b[:], in_=wgo[:, 256:512])
+
+        u_codes, u_scales = quantise(u_raw, "u", 80)
+        banks = [ps.tile([M, N], F32, name="bank%d" % s) for s in range(S // N)]
+
+        def multiply(key, on_vector):
+            a, c0 = key
+            codes, scales = quantise(raws[key], "%d_%d" % key, on_vector)
+            for off in range(0, raws[key].shape[2], N):
+                if a == 0:
+                    lhsT, lhsT_scale = u_codes[:].bitcast(FP8X4), u_scales[:]
+                else:
+                    lhsT, lhsT_scale = w4[:, a - 1, :].bitcast(FP4X4), w4_plane[:, a - 1, :]
+                nc.tensor.matmul_mx(
+                    out=banks[(c0 + off) // N][:],
+                    lhsT=lhsT,
+                    lhsT_scale=lhsT_scale,
+                    rhs=codes[:, off : off + N].bitcast(FP8X4),
+                    rhs_scale=scales[:, off : off + N],
+                    start=(a == 0),
+                    stop=(a == X_PASSES),
+                )
+
+        def place(s, weights, act):
+            if act is None:
+                act = sb.tile([P, N], F32, name="act%d" % s)
+                act = act[:]
+            nc.scalar.activation(act, banks[s][:], SILU, bias=bias[:])
+            nc.vector.tensor_tensor(
+                placed[:].indirect(offsets[:, s * N // 16 : (s + 1) * N // 16]), act, weights, mybir.AluOpType.mult
+            )
+
+        multiply((0, 0), 160)
+        multiply((1, 0), 160)
+        multiply((2, 0), 160)
+        multiply((3, 0), 160)
+        place(0, wgo_a[:, 0:128], None)
+        place(1, wgo_a[:, 128:256], None)
+        multiply((0, 256), 0)
+        multiply((1, 256), 160)
+        multiply((2, 256), 0)
+        multiply((3, 256), 0)
+        multiply((2, 384), 64)
+        multiply((3, 384), 64)
+        place(2, wgo_b[:, 0:128], raws[(3, 384)][:, 0, :])
+        place(3, wgo_b[:, 128:256], None)
+        nc.sync.dma_start(out=out, in_=placed[:])

@@ -20,7 +20,7 @@ PACK = 4
 K_PASS = P * PACK
 X_PASSES = K // K_PASS
 N = 128
-RUN = 4
+RUN = 2
 
 
 def tile_list_hscat_d_silu_kernel(tc, x, w4_words, w4_scales, c, u, b, wgo, offs, out):
@@ -60,25 +60,23 @@ def tile_list_hscat_d_silu_kernel(tc, x, w4_words, w4_scales, c, u, b, wgo, offs
 
         raws = {}
         u_raw = load_rows(u, "u")
-        raws[(0, 0)] = load_rows(c[:, 0:256], "0_0")
-        raws[(1, 0)] = load_rows(x_rows(0, 0, 256), "1_0")
+        raws[(0, 0)] = load_rows(c[:, 0:512], "0_0")
         for q in range(4):
             nc.sync.dma_start(
                 out=w4_plane[32 * q : 32 * q + 4, :, :].bitcast(I32),
                 in_=w4_scales[:, 4 * q : 4 * q + 4, :].rearrange("a r n -> r a n").bitcast(I32),
             )
+        raws[(1, 0)] = load_rows(x_rows(0, 0, 512), "1_0")
         raws[(2, 0)] = load_rows(x_rows(1, 0, 256), "2_0")
-        raws[(3, 0)] = load_rows(x_rows(2, 0, 256), "3_0")
         w4 = sb.tile([P, X_PASSES, 2 * M], U8, name="w4", align_bytes=64)
         nc.sync.dma_start(out=w4[:].bitcast(I32), in_=w4_words.rearrange("a p n -> p a n").bitcast(I32))
+        raws[(3, 0)] = load_rows(x_rows(2, 0, 256), "3_0")
         bias = sb.tile([P, 1], F32, name="bias")
         nc.sync.dma_start(out=bias[:], in_=b.rearrange("(p o) -> p o", o=1))
         offsets = sb.tile([P, S // 16], U16, name="offsets")
         nc.sync.dma_start(offsets[:], offs)
         wgo_a = sb.tile([P, 256], F32, name="wgo_a")
         nc.sync.dma_start(out=wgo_a[:], in_=wgo[:, 0:256])
-        raws[(0, 256)] = load_rows(c[:, 256:512], "0_256")
-        raws[(1, 256)] = load_rows(x_rows(0, 256, 512), "1_256")
         raws[(2, 256)] = load_rows(x_rows(1, 256, 384), "2_256")
         raws[(3, 256)] = load_rows(x_rows(2, 256, 384), "3_256")
         raws[(2, 384)] = load_rows(x_rows(1, 384, 512), "2_384")
@@ -116,18 +114,16 @@ def tile_list_hscat_d_silu_kernel(tc, x, w4_words, w4_scales, c, u, b, wgo, offs
                 placed[:].indirect(offsets[:, s * N // 16 : (s + 1) * N // 16]), act, weights, mybir.AluOpType.mult
             )
 
-        multiply((0, 0), 160)
-        multiply((1, 0), 160)
+        multiply((0, 0), 320)
+        multiply((1, 0), 320)
         multiply((2, 0), 160)
         multiply((3, 0), 160)
-        place(0, wgo_a[:, 0:128], None)
-        place(1, wgo_a[:, 128:256], None)
-        multiply((0, 256), 0)
-        multiply((1, 256), 160)
-        multiply((2, 256), 0)
+        multiply((2, 256), 80)
+        place(0, wgo_a[:, 0:128], raws[(2, 256)][:, 0, :])
         multiply((3, 256), 0)
-        multiply((2, 384), 64)
-        multiply((3, 384), 64)
+        place(1, wgo_a[:, 128:256], raws[(3, 256)][:, 0, :])
+        multiply((2, 384), 0)
+        multiply((3, 384), 0)
         place(2, wgo_b[:, 0:128], raws[(3, 384)][:, 0, :])
         place(3, wgo_b[:, 128:256], None)
         nc.sync.dma_start(out=out, in_=placed[:])

@@ -70,13 +70,14 @@ def tile_list_hscat_d_silu_kernel(tc, x, w4_words, w4_scales, c, u, b, wgo, offs
         raws[(2, 0)] = load_rows(x_rows(1, 0, 256), "2_0")
         w4 = sb.tile([P, X_PASSES, 2 * M], U8, name="w4", align_bytes=64)
         nc.sync.dma_start(out=w4[:].bitcast(I32), in_=w4_words.rearrange("a p n -> p a n").bitcast(I32))
-        raws[(3, 0)] = load_rows(x_rows(2, 0, 256), "3_0")
+        raws[(3, 0)] = load_rows(x_rows(2, 0, 128), "3_0")
         bias = sb.tile([P, 1], F32, name="bias")
         nc.sync.dma_start(out=bias[:], in_=b.rearrange("(p o) -> p o", o=1))
         offsets = sb.tile([P, S // 16], U16, name="offsets")
         nc.sync.dma_start(offsets[:], offs)
         wgo_a = sb.tile([P, 256], F32, name="wgo_a")
         nc.sync.dma_start(out=wgo_a[:], in_=wgo[:, 0:256])
+        raws[(3, 128)] = load_rows(x_rows(2, 128, 256), "3_128")
         raws[(2, 256)] = load_rows(x_rows(1, 256, 384), "2_256")
         raws[(3, 256)] = load_rows(x_rows(2, 256, 384), "3_256")
         raws[(2, 384)] = load_rows(x_rows(1, 384, 512), "2_384")
@@ -117,12 +118,13 @@ def tile_list_hscat_d_silu_kernel(tc, x, w4_words, w4_scales, c, u, b, wgo, offs
         multiply((0, 0), 320)
         multiply((1, 0), 320)
         multiply((2, 0), 160)
-        multiply((3, 0), 160)
-        multiply((2, 256), 80)
-        place(0, wgo_a[:, 0:128], raws[(2, 256)][:, 0, :])
+        multiply((3, 0), 0)
+        multiply((3, 128), 80)
+        place(0, wgo_a[:, 0:128], raws[(3, 128)][:, 0, :])
+        multiply((2, 256), 0)
         multiply((3, 256), 0)
         place(1, wgo_a[:, 128:256], raws[(3, 256)][:, 0, :])
-        multiply((2, 384), 0)
+        multiply((2, 384), 80)
         multiply((3, 384), 0)
         place(2, wgo_b[:, 0:128], raws[(3, 384)][:, 0, :])
         place(3, wgo_b[:, 128:256], None)

from contextlib import ExitStack

import concourse.mybir as mybir

K, L, M, T, S = 1536, 512, 128, 1024, 512
FLOPS = 2 * (K + L) * M * S

F32 = mybir.dt.float32
BF16 = mybir.dt.bfloat16
I32 = mybir.dt.int32
U32 = mybir.dt.uint32
U16 = mybir.dt.uint16
U8 = mybir.dt.uint8
FP8X4 = mybir.dt.float8_e4m3fn_x4
FP4X4 = mybir.dt.float4_e2m1fn_x4
SILU = mybir.ActivationFunctionType.Silu

P = 128
PACK = 4
K_PASS = P * PACK
X_PASSES = K // K_PASS
N = 128
RUN = 2


def tile_list_hscat_d_silu_kernel(tc, x, w4_words, w4_scales, c, u, b, wgo, offs, out):
    nc = tc.nc
    with ExitStack() as ctx:
        sb = ctx.enter_context(tc.tile_pool(name="sb", bufs=1))
        ps = ctx.enter_context(tc.psum_pool(name="ps", bufs=1))

        def load_rows(rows, name):
            raw = sb.tile([P, PACK, rows.shape[1]], F32, name="raw_" + name, align_bytes=64)
            nc.sync.dma_start(out=raw[:], in_=rows.rearrange("(p t) w -> p t w", t=PACK))
            return raw

        def quantise(raw, name, on_vector):
            width = raw.shape[2]
            woven = sb.tile([P, width * PACK], BF16, name="woven_" + name, align_bytes=64)
            for copy, c0, c1 in ((nc.vector.tensor_copy, 0, on_vector), (nc.scalar.copy, on_vector, width)):
                if c1 > c0:
                    copy(
                        out=woven[:, c0 * PACK : c1 * PACK].rearrange("p (w i t) -> p w t i", i=RUN, t=PACK),
                        in_=raw[:, :, c0:c1].rearrange("p t (w i) -> p w t i", i=RUN),
                    )
            codes = sb.tile([P, width], U32, name="codes_" + name, align_bytes=64)
            scales = sb.tile([P, width], U8, name="scales_" + name, align_bytes=64)
            nc.vector.quantize_mx(out=codes[:].bitcast(FP8X4), scales=scales[:], in_=woven[:])
            return codes, scales

        w4_plane = sb.tile([P, X_PASSES, M], U8, name="w4_plane", align_bytes=64)
        nc.vector.memset(w4_plane[:].bitcast(I32), 0)
        placed = sb.tile([P, T], F32, name="placed")
        nc.vector.memset(placed[:], 0.0)
        warm = sb.tile([P, 1], F32, name="warm")
        nc.scalar.activation(warm[:], placed[:, 0:1], SILU)

        def x_rows(a, c0, c1):
            return x[a * K_PASS : (a + 1) * K_PASS, c0:c1]

        raws = {}
        u_raw = load_rows(u, "u")
        raws[(0, 0)] = load_rows(c[:, 0:512], "0_0")
        for q in range(4):
            nc.sync.dma_start(
                out=w4_plane[32 * q : 32 * q + 4, :, :].bitcast(I32),
                in_=w4_scales[:, 4 * q : 4 * q + 4, :].rearrange("a r n -> r a n").bitcast(I32),
            )
        raws[(1, 0)] = load_rows(x_rows(0, 0, 512), "1_0")
        raws[(2, 0)] = load_rows(x_rows(1, 0, 256), "2_0")
        w4 = sb.tile([P, X_PASSES, 2 * M], U8, name="w4", align_bytes=64)
        nc.sync.dma_start(out=w4[:].bitcast(I32), in_=w4_words.rearrange("a p n -> p a n").bitcast(I32))
        raws[(3, 0)] = load_rows(x_rows(2, 0, 128), "3_0")
        bias = sb.tile([P, 1], F32, name="bias")
        nc.sync.dma_start(out=bias[:], in_=b.rearrange("(p o) -> p o", o=1))
        offsets = sb.tile([P, S // 16], U16, name="offsets")
        nc.sync.dma_start(offsets[:], offs)
        wgo_a = sb.tile([P, 256], F32, name="wgo_a")
        nc.sync.dma_start(out=wgo_a[:], in_=wgo[:, 0:256])
        raws[(3, 128)] = load_rows(x_rows(2, 128, 256), "3_128")
        raws[(2, 256)] = load_rows(x_rows(1, 256, 384), "2_256")
        raws[(3, 256)] = load_rows(x_rows(2, 256, 384), "3_256")
        raws[(2, 384)] = load_rows(x_rows(1, 384, 512), "2_384")
        raws[(3, 384)] = load_rows(x_rows(2, 384, 512), "3_384")
        wgo_b = sb.tile([P, 256], F32, name="wgo_b")
        nc.sync.dma_start(out=wgo_b[:], in_=wgo[:, 256:512])

        u_codes, u_scales = quantise(u_raw, "u", 80)
        banks = [ps.tile([M, N], F32, name="bank%d" % s) for s in range(S // N)]

        def multiply(key, on_vector):
            a, c0 = key
            codes, scales = quantise(raws[key], "%d_%d" % key, on_vector)
            for off in range(0, raws[key].shape[2], N):
                if a == 0:
                    lhsT, lhsT_scale = u_codes[:].bitcast(FP8X4), u_scales[:]
                else:
                    lhsT, lhsT_scale = w4[:, a - 1, :].bitcast(FP4X4), w4_plane[:, a - 1, :]
                nc.tensor.matmul_mx(
                    out=banks[(c0 + off) // N][:],
                    lhsT=lhsT,
                    lhsT_scale=lhsT_scale,
                    rhs=codes[:, off : off + N].bitcast(FP8X4),
                    rhs_scale=scales[:, off : off + N],
                    start=(a == 0),
                    stop=(a == X_PASSES),
                )

        def place(s, weights, act):
            if act is None:
                act = sb.tile([P, N], F32, name="act%d" % s)
                act = act[:]
            nc.scalar.activation(act, banks[s][:], SILU, bias=bias[:])
            nc.vector.tensor_tensor(
                placed[:].indirect(offsets[:, s * N // 16 : (s + 1) * N // 16]), act, weights, mybir.AluOpType.mult
            )

        multiply((0, 0), 320)
        multiply((1, 0), 320)
        multiply((2, 0), 160)
        multiply((3, 0), 0)
        multiply((3, 128), 80)
        place(0, wgo_a[:, 0:128], raws[(3, 128)][:, 0, :])
        multiply((2, 256), 0)
        multiply((3, 256), 0)
        place(1, wgo_a[:, 128:256], raws[(3, 256)][:, 0, :])
        multiply((2, 384), 80)
        multiply((3, 384), 0)
        place(2, wgo_b[:, 0:128], raws[(3, 384)][:, 0, :])
        place(3, wgo_b[:, 128:256], None)
        nc.sync.dma_start(out=out, in_=placed[:])
